import numpy as np
import ml_dtypes


def mxq(x, axis, fmt="e4m3"):
    dtype, down = {"e4m3": (ml_dtypes.float8_e4m3fn, 7), "e5m2": (ml_dtypes.float8_e5m2, 14)}[fmt]
    v = np.moveaxis(np.asarray(x, np.float32).astype(ml_dtypes.bfloat16).astype(np.float64), axis, -1)
    blocks = v.reshape(v.shape[:-1] + (-1, 32))
    amax = np.abs(blocks).max(-1, keepdims=True)
    byte = np.maximum(np.where(amax > 0, np.frexp(amax)[1] - 1 + 127, 0) - down, 1)
    scale = np.exp2(byte - 127.0)
    codes = (blocks / scale).astype(np.float32).astype(dtype).astype(np.float64)
    return np.moveaxis((codes * scale).reshape(v.shape), -1, axis)


WIDE = False


def mx_kscale(k):
    if not WIDE:
        return np.ones(k)
    levels = np.array([10, -10, 5, -5, 0])
    if k % 512:
        return np.exp2(np.random.permutation(np.resize(levels, k // 32))).repeat(32)
    a = np.empty((k // 512, 16))
    for p in range(k // 512):
        a[p, :8] = np.random.permutation(np.resize(levels, 8))
        for g in range(8):
            far = levels[np.abs(levels - a[p, g]) >= 10]
            a[p, g + 8] = far[np.random.randint(len(far))]
    return np.exp2(a.ravel()).repeat(32)


def f64(x):
    return np.asarray(x).astype(np.float64)


def striped(idx):
    return np.tile(np.asarray(idx).reshape(-1, 16).T, (8, 1)).astype(np.uint16)


def unstriped(offs):
    return offs[:16].T.reshape(-1).astype(np.int64)


E2M1 = np.array([0.0, 0.5, 1.0, 1.5, 2.0, 3.0, 4.0, 6.0, -0.0, -0.5, -1.0, -1.5, -2.0, -3.0, -4.0, -6.0])


def pack_weight(w, fmt):
    k, n = w.shape
    w = f64(np.asarray(w, np.float32).astype(ml_dtypes.bfloat16)).reshape(k // 32, 32, n)
    amax = np.abs(w).max(1)
    if fmt == "e4m3":
        byte = np.frexp(amax)[1] - 1 + 127 - 7
    else:
        mant, ex = np.frexp(amax / 6.0)
        byte = np.where(mant > 0.5, ex, ex - 1) + 127
    byte = np.clip(np.where(amax > 0, byte, 1), 1, 254)
    scaled = (w * np.exp2(127.0 - byte)[:, None, :]).reshape(k, n).astype(np.float32)
    by_word = np.ascontiguousarray(scaled.reshape(k // 512, 128, 4, n).transpose(0, 1, 3, 2))
    if fmt == "e4m3":
        words = by_word.astype(ml_dtypes.float8_e4m3fn).view(np.uint8)
    else:
        c = by_word.astype(ml_dtypes.float4_e2m1fn).view(np.uint8) & 0xF
        words = (c[..., 0::2] | (c[..., 1::2] << 4)).reshape(k // 512, 128, 2 * n)
    return np.ascontiguousarray(words), np.ascontiguousarray(byte.astype(np.uint8).reshape(k // 512, 16, n))


def unpack_weight(words, scales, fmt):
    g, _, n = scales.shape
    words = np.ascontiguousarray(words).reshape(g, 128, n, -1)
    if fmt == "e4m3":
        vals = words.view(ml_dtypes.float8_e4m3fn).astype(np.float64)
    else:
        nib = np.empty((g, 128, n, 4), np.uint8)
        nib[..., 0::2] = words & 0xF
        nib[..., 1::2] = words >> 4
        vals = E2M1[nib]
    vals = vals * np.repeat(np.exp2(scales.astype(np.float64) - 127.0), 8, axis=1)[..., None]
    return vals.transpose(0, 1, 3, 2).reshape(g * 512, n)


def bf(x):
    return np.asarray(x, np.float32).astype(ml_dtypes.bfloat16)


def planes(Y):
    r, m = Y.shape
    b = f64(bf(Y)).reshape(r // 32, 32, m)
    amax = np.abs(b).max(1)
    byte = np.clip(np.where(amax > 0, np.frexp(amax)[1] - 1 + 127 - 7, 1), 1, 254)
    codes = (b * np.exp2(127.0 - byte)[:, None, :]).reshape(r, m).astype(np.float32).astype(ml_dtypes.float8_e4m3fn).view(np.uint8)
    words = codes.reshape(r // 512, 128, 4, m).transpose(0, 1, 3, 2)
    return np.ascontiguousarray(words), np.ascontiguousarray(byte.astype(np.uint8).reshape(r // 512, 16, m))


K, T, J, I, S, R, N = 1024, 2048, 1024, 512, 1024, 512, 512


def setup_inputs():
    n = np.random.standard_normal
    idx = np.random.permutation(T)[:J]
    idx2 = np.random.permutation(J)[:I]
    idx3 = np.random.permutation(S)[:I]
    fk = mx_kscale(K)
    fr = mx_kscale(R)
    xtp = pack_weight(n((K, T)) / fk[:, None], "e2m1")
    wap = pack_weight(n((K, R)) * 1 / np.sqrt(K) * fk[:, None] * fr, "e4m3")
    wbp = pack_weight(n((R, N)) * 1 / np.sqrt(R) / fr[:, None], "e2m1")
    return {
        "xt_words": xtp[0],
        "xt_scales": xtp[1],
        "wa_words": wap[0],
        "wa_scales": wap[1],
        "wb_words": wbp[0],
        "wb_scales": wbp[1],
        "old": (1.0 * n((N, S))).astype(np.float32),
        "offs": striped(idx),
        "offs2": striped(idx2),
        "offs3": striped(idx3),
    }


def reference(xt_words, xt_scales, wa_words, wa_scales, wb_words, wb_scales, old, offs, offs2, offs3):
    idx = unstriped(offs)
    idx2 = unstriped(offs2)
    idx3 = unstriped(offs3)
    xtu = unpack_weight(xt_words, xt_scales, "e2m1")
    wau = unpack_weight(wa_words, wa_scales, "e4m3")
    wbu = unpack_weight(wb_words, wb_scales, "e2m1")
    xtidxg = xtu[:, idx]
    a = wau.T @ xtidxg
    hid = np.maximum(a, 0.0)
    hididx2q = mxq(hid[:, idx2], 0, "e4m3")
    p = wbu.T @ hididx2q
    pp = np.zeros((N, S))
    pp[:, idx3] = p
    y = pp + 0.3 * f64(old)
    words, scales = planes(y)
    return y, words, scales

@@ -1,0 +1,227 @@
+from contextlib import ExitStack
+
+import concourse.mybir as mybir
+
+K, T, J, I, S, R, N = 1024, 2048, 1024, 512, 1024, 512, 512
+FLOPS = 2 * K * R * J + 2 * R * N * I
+
+F32 = mybir.dt.float32
+BF16 = mybir.dt.bfloat16
+I32 = mybir.dt.int32
+U32 = mybir.dt.uint32
+U16 = mybir.dt.uint16
+U8 = mybir.dt.uint8
+FP8X4 = mybir.dt.float8_e4m3fn_x4
+FP4X4 = mybir.dt.float4_e2m1fn_x4
+MULT = mybir.AluOpType.mult
+ADD = mybir.AluOpType.add
+RELU = mybir.ActivationFunctionType.Relu
+
+P = 128
+PACK = 4
+QUADS = 4
+PASSES = K // (P * PACK)
+JH = 512
+IH = 256
+LIST = 16
+
+
+def tile_moe_expert_relay_scattered_pl_kernel(
+    tc, xt_words, xt_scales, wa_words, wa_scales, wb_words, wb_scales, old, offs, offs2, offs3, out_0, out_1, out_2
+):
+    nc = tc.nc
+    with ExitStack() as ctx:
+        lists = ctx.enter_context(tc.tile_pool(name="lists", bufs=1))
+        keep = ctx.enter_context(tc.tile_pool(name="keep", bufs=1))
+        psum = ctx.enter_context(tc.psum_pool(name="psum", bufs=1))
+
+        o1 = lists.tile([P, J // LIST], U16, name="o1")
+        o2 = lists.tile([P, I // LIST], U16, name="o2")
+        o3 = lists.tile([P, I // LIST], U16, name="o3")
+
+        xs = keep.tile([P, T], U8, name="xs", tag="xs_then_wb", align_bytes=64)
+        xw = [keep.tile([P, T], U16, name="xw%d" % z, tag="xw%d" % z, align_bytes=64) for z in range(PASSES)]
+        wa_raw = keep.tile([P, PASSES, R], I32, name="wa_raw", align_bytes=64)
+        was_raw = keep.tile([P, PASSES, R], U8, name="was_raw", tag="was_then_xg", align_bytes=64)
+        sg = keep.tile([P, J], U8, name="sg", align_bytes=64)
+        planes = keep.tile([P, PASSES * J], U8, name="planes", align_bytes=64)
+
+        nc.vector.memset(was_raw[:].bitcast(I32), 0)
+        nc.vector.memset(xs[32:64, :].bitcast(I32), 0)
+        nc.vector.memset(xs[64:128, :].bitcast(I32), 0)
+        nc.vector.memset(planes[:].bitcast(I32), 0)
+
+        nc.sync.dma_start(o1[:], offs)
+        nc.sync.dma_start(xs[0:32, :].bitcast(I32), xt_scales.rearrange("z q c -> (z q) c").bitcast(I32))
+        nc.sync.dma_start(wa_raw[:], wa_words.rearrange("z p n t -> p z (n t)").bitcast(I32))
+        for z in range(PASSES):
+            nc.sync.dma_start(xw[z][:].bitcast(I32), xt_words[z].bitcast(I32))
+        for q in range(QUADS):
+            nc.sync.dma_start(
+                was_raw[32 * q : 32 * q + 4, :, :].bitcast(I32),
+                wa_scales[:, 4 * q : 4 * q + 4, :].rearrange("z q c -> q z c").bitcast(I32),
+            )
+        nc.sync.dma_start(o2[:], offs2)
+        nc.sync.dma_start(o3[:], offs3)
+
+        nc.vector.tensor_copy(sg[:], xs[:].indirect(o1[:]))
+        for z in range(PASSES):
+            for q in range(QUADS):
+                row = 16 * z + 4 * q
+                nc.scalar.dma_start(planes[32 * q : 32 * q + 4, z * J : (z + 1) * J].bitcast(I32), sg[row : row + 4, :].bitcast(I32))
+
+        wb_both = keep.tile([P, 3 * N], U8, name="wb_both", tag="xs_then_wb", align_bytes=64)
+        nc.vector.memset(wb_both[:, 2 * N :].bitcast(I32), 0)
+        nc.sync.dma_start(wb_both[:, : 2 * N].bitcast(I32), wb_words[0].bitcast(I32))
+        for q in range(QUADS):
+            nc.sync.dma_start(
+                wb_both[32 * q : 32 * q + 4, 2 * N :].bitcast(I32), wb_scales[0, 4 * q : 4 * q + 4, :].bitcast(I32)
+            )
+
+        xg = {}
+        wa = keep.tile([P, PASSES, R], I32, name="wa", align_bytes=64)
+        was = keep.tile([P, PASSES, R], U8, name="was", align_bytes=64)
+        wb = keep.tile([P, N], U16, name="wb", align_bytes=64)
+        wbs = keep.tile([P, N], U8, name="wbs", align_bytes=64)
+        hid = [keep.tile([P, J], F32, name="hid%d" % t, tag="hid%d" % t, align_bytes=64) for t in range(PACK)]
+
+        def gather_words(h, z, into):
+            cols = slice(h * JH // LIST, (h + 1) * JH // LIST)
+            xg[h, z] = into
+            nc.vector.tensor_copy(into, xw[z][:].indirect(o1[:, cols]))
+
+        def first_layer(h, groups):
+            banks = [psum.tile([P, JH], F32, name="a%d%d" % (t, h), tag="bank%d%d" % (t, h)) for t in range(PACK)]
+            for group in groups:
+                for z, t in [(z, t) for z in range(PASSES) for t in group]:
+                    cols = slice(t * P, (t + 1) * P)
+                    nc.tensor.matmul_mx(
+                        out=banks[t][:],
+                        lhsT=wa[:, z, cols].bitcast(FP8X4),
+                        lhsT_scale=was[:, z, cols],
+                        rhs=xg[h, z].bitcast(FP4X4),
+                        rhs_scale=planes[:, z * J + h * JH : z * J + (h + 1) * JH],
+                        start=(z == 0),
+                        stop=(z == PASSES - 1),
+                    )
+            for t in range(PACK):
+                nc.scalar.activation(hid[t][:, h * JH : (h + 1) * JH], banks[t][:], RELU)
+
+        xg_first = keep.tile([P, JH], U16, name="xg_first", align_bytes=64)
+        gather_words(0, 0, xg_first[:])
+        nc.vector.tensor_copy(
+            wa[:].rearrange("p z (t m) -> p z m t", t=PACK), wa_raw[:].rearrange("p z (m t) -> p z m t", t=PACK)
+        )
+        nc.vector.tensor_copy(
+            was[:].rearrange("p z (t m) -> p z t m", t=PACK), was_raw[:].rearrange("p z (m t) -> p z t m", t=PACK)
+        )
+        xg_rest = keep.tile([P, 3 * JH], U16, name="xg_rest", tag="was_then_xg", align_bytes=64)
+        gather_words(0, 1, xg_rest[:, :JH])
+        first_layer(0, [(0, 1), (2, 3)])
+        gather_words(1, 0, xg_rest[:, JH : 2 * JH])
+        gather_words(1, 1, xg_rest[:, 2 * JH :])
+        first_layer(1, [(t,) for t in range(PACK)])
+        for dealt, raw in ((wb, wb_both[:, : 2 * N].bitcast(U16)), (wbs, wb_both[:, 2 * N :])):
+            nc.vector.tensor_copy(
+                dealt[:].rearrange("p (t m) -> p t m", t=PACK), raw.rearrange("p (m t) -> p t m", t=PACK)
+            )
+
+        old4 = keep.tile([P, PACK, S], F32, name="old4", tag="xw0", align_bytes=64)
+        nc.sync.dma_start(old4[:], old.rearrange("(p t) s -> p t s", t=PACK))
+
+        g4 = [keep.tile([P, PACK, IH], F32, name="g4%d" % h, align_bytes=64) for h in range(2)]
+        hb = [keep.tile([P, IH, PACK], BF16, name="hb%d" % h, tag="hb%d" % h, align_bytes=64) for h in range(2)]
+        hq = [keep.tile([P, IH], U32, name="hq%d" % h, align_bytes=64) for h in range(2)]
+        hs = [keep.tile([P, IH], U8, name="hs%d" % h, align_bytes=64) for h in range(2)]
+        ps = [keep.tile([P, I], F32, name="ps%d" % t, align_bytes=64) for t in range(PACK)]
+
+        def gather_hid(h, t):
+            cols = slice(h * IH // LIST, (h + 1) * IH // LIST)
+            nc.vector.tensor_copy(g4[h][:, t, :], hid[t][:].indirect(o2[:, cols]))
+
+        def weave(h):
+            nc.scalar.copy(
+                hb[h][:].rearrange("p (c i) t -> p c t i", i=4), g4[h][:].rearrange("p t (c i) -> p c t i", i=4)
+            )
+
+        def quantise(h):
+            nc.vector.quantize_mx(out=hq[h][:].bitcast(FP8X4), scales=hs[h][:], in_=hb[h][:].rearrange("p i t -> p (i t)"))
+
+        def second_layer(h, t):
+            cols = slice(t * P, (t + 1) * P)
+            bank = psum.tile([P, IH], F32, name="b%d%d" % (t, h), tag="bank%d%d" % (t, h))
+            nc.tensor.matmul_mx(
+                out=bank[:],
+                lhsT=wb[:, cols].bitcast(FP4X4),
+                lhsT_scale=wbs[:, cols],
+                rhs=hq[h][:].bitcast(FP8X4),
+                rhs_scale=hs[h][:],
+                start=True,
+                stop=True,
+            )
+            nc.scalar.copy(ps[t][:, h * IH : (h + 1) * IH], bank[:])
+
+        def scatter(t, lo, hi):
+            nc.vector.tensor_copy(pp[t][:].indirect(o3[:, lo // LIST : hi // LIST]), ps[t][:, lo:hi])
+
+        y4 = keep.tile([P, PACK, S], F32, name="y4", align_bytes=64)
+        out_rows = out_0.rearrange("(p t) s -> p t s", t=PACK)
+
+        def add_old(t, lo, hi):
+            nc.vector.scalar_tensor_tensor(y4[:, t, lo:hi], old4[:, t, lo:hi], 0.3, pp[t][:, lo:hi], MULT, ADD)
+
+        for t in range(PACK):
+            gather_hid(0, t)
+        weave(0)
+        for t in range(PACK - 1):
+            gather_hid(1, t)
+        quantise(0)
+        gather_hid(1, PACK - 1)
+        pp = []
+        for t in range(PACK):
+            pp.append(keep.tile([P, S], F32, name="pp%d" % t, tag=["pp0", "pp1", "hid3", "hb0"][t], align_bytes=64))
+            nc.vector.memset(pp[t][:], 0.0)
+        second_layer(0, 0)
+        second_layer(0, 1)
+        weave(1)
+        second_layer(0, 2)
+        second_layer(0, 3)
+        scatter(0, 0, IH)
+        quantise(1)
+        for t in range(PACK):
+            second_layer(1, t)
+        scatter(1, 0, IH)
+        scatter(0, IH, I)
+        scatter(1, IH, I)
+        add_old(0, 0, S)
+        nc.sync.dma_start(out_rows[:, 0, :], y4[:, 0, :])
+        scatter(2, 0, I)
+        add_old(1, 0, S)
+        nc.sync.dma_start(out_rows[:, 1, :], y4[:, 1, :])
+
+        yb = keep.tile([P, S, PACK], BF16, name="yb", align_bytes=64)
+        yq = keep.tile([P, S], U32, name="yq", align_bytes=64)
+        ys = keep.tile([P, S], U8, name="ys", align_bytes=64)
+
+        def weave_pair(engine_copy, t0, lo, hi):
+            engine_copy(yb[:, lo:hi, t0 : t0 + 2], y4[:, t0 : t0 + 2, lo:hi].rearrange("p t s -> p s t"))
+
+        weave_pair(nc.scalar.copy, 0, 0, S)
+        scatter(3, 0, I)
+        add_old(2, 0, S)
+        nc.sync.dma_start(out_rows[:, 2, :], y4[:, 2, :])
+        half = S // 2
+        split = 384
+        add_old(3, 0, half)
+        add_old(3, half, S)
+        nc.sync.dma_start(out_rows[:, 3, :], y4[:, 3, :])
+        weave_pair(nc.scalar.copy, 2, 0, split)
+        weave_pair(nc.vector.tensor_copy, 2, split, S)
+        words = out_1[0].rearrange("p s t -> p (s t)").bitcast(I32)
+        for lo, hi in ((half, S), (0, half)):
+            nc.vector.quantize_mx(
+                out=yq[:, lo:hi].bitcast(FP8X4), scales=ys[:, lo:hi], in_=yb[:, lo:hi, :].rearrange("p s t -> p (s t)")
+            )
+            nc.sync.dma_start(words[:, lo:hi], yq[:, lo:hi].bitcast(I32))
+        for q in range(QUADS):
+            nc.scalar.dma_start(out_2[0, 4 * q : 4 * q + 4, :].bitcast(I32), ys[32 * q : 32 * q + 4, :].bitcast(I32))

@@ -15,6 +15,7 @@ FP8X4 = mybir.dt.float8_e4m3fn_x4
 FP4X4 = mybir.dt.float4_e2m1fn_x4
 MULT = mybir.AluOpType.mult
 ADD = mybir.AluOpType.add
+COPY = mybir.ActivationFunctionType.Copy
 RELU = mybir.ActivationFunctionType.Relu
 
 P = 128
@@ -39,17 +40,21 @@ def tile_moe_expert_relay_scattered_pl_kernel(
         o2 = lists.tile([P, I // LIST], U16, name="o2")
         o3 = lists.tile([P, I // LIST], U16, name="o3")
 
-        xs = keep.tile([P, T], U8, name="xs", tag="xs_then_wb", align_bytes=64)
+        xs = keep.tile([P, T], U8, name="xs", align_bytes=64)
         xw = [keep.tile([P, T], U16, name="xw%d" % z, tag="xw%d" % z, align_bytes=64) for z in range(PASSES)]
-        wa_raw = keep.tile([P, PASSES, R], I32, name="wa_raw", align_bytes=64)
+        wa_raw = keep.tile([P, PASSES, R], I32, name="wa_raw", tag="wa_then_wb", align_bytes=64)
         was_raw = keep.tile([P, PASSES, R], U8, name="was_raw", tag="was_then_xg", align_bytes=64)
         sg = keep.tile([P, J], U8, name="sg", align_bytes=64)
         planes = keep.tile([P, PASSES * J], U8, name="planes", align_bytes=64)
 
-        nc.vector.memset(was_raw[:].bitcast(I32), 0)
-        nc.vector.memset(xs[32:64, :].bitcast(I32), 0)
-        nc.vector.memset(xs[64:128, :].bitcast(I32), 0)
-        nc.vector.memset(planes[:].bitcast(I32), 0)
+        nc.gpsimd.memset(was_raw[:].bitcast(I32), 0)
+        nc.gpsimd.memset(xs[32:64, :].bitcast(I32), 0)
+        nc.gpsimd.memset(xs[64:128, :].bitcast(I32), 0)
+        pp = [keep.tile([P, S], F32, name="pp%d" % t, align_bytes=64) for t in range(PACK - 1)]
+        nc.gpsimd.memset(pp[0][:], 0.0)
+        nc.gpsimd.memset(pp[1][:], 0.0)
+        nc.gpsimd.memset(planes[:].bitcast(I32), 0)
+        nc.gpsimd.memset(pp[2][:], 0.0)
 
         nc.sync.dma_start(o1[:], offs)
         nc.sync.dma_start(xs[0:32, :].bitcast(I32), xt_scales.rearrange("z q c -> (z q) c").bitcast(I32))
@@ -65,25 +70,19 @@ def tile_moe_expert_relay_scattered_pl_kernel(
         nc.sync.dma_start(o3[:], offs3)
 
         nc.vector.tensor_copy(sg[:], xs[:].indirect(o1[:]))
-        for z in range(PASSES):
-            for q in range(QUADS):
-                row = 16 * z + 4 * q
-                nc.scalar.dma_start(planes[32 * q : 32 * q + 4, z * J : (z + 1) * J].bitcast(I32), sg[row : row + 4, :].bitcast(I32))
-
-        wb_both = keep.tile([P, 3 * N], U8, name="wb_both", tag="xs_then_wb", align_bytes=64)
-        nc.vector.memset(wb_both[:, 2 * N :].bitcast(I32), 0)
-        nc.sync.dma_start(wb_both[:, : 2 * N].bitcast(I32), wb_words[0].bitcast(I32))
         for q in range(QUADS):
-            nc.sync.dma_start(
-                wb_both[32 * q : 32 * q + 4, 2 * N :].bitcast(I32), wb_scales[0, 4 * q : 4 * q + 4, :].bitcast(I32)
-            )
+            for z in range(PASSES):
+                row = 16 * z + 4 * q
+                nc.sync.dma_start(planes[32 * q : 32 * q + 4, z * J : (z + 1) * J].bitcast(I32), sg[row : row + 4, :].bitcast(I32))
 
         xg = {}
         wa = keep.tile([P, PASSES, R], I32, name="wa", align_bytes=64)
         was = keep.tile([P, PASSES, R], U8, name="was", align_bytes=64)
         wb = keep.tile([P, N], U16, name="wb", align_bytes=64)
         wbs = keep.tile([P, N], U8, name="wbs", align_bytes=64)
-        hid = [keep.tile([P, J], F32, name="hid%d" % t, tag="hid%d" % t, align_bytes=64) for t in range(PACK)]
+        hid = [keep.tile([P, J], F32, name="hid%d" % t, align_bytes=64)[:] for t in range(PACK - 1)]
+        last = keep.tile([P, J + PACK * IH], F32, name="last", align_bytes=64)
+        hid.append(last[:, :J])
 
         def gather_words(h, z, into):
             cols = slice(h * JH // LIST, (h + 1) * JH // LIST)
@@ -91,7 +90,7 @@ def tile_moe_expert_relay_scattered_pl_kernel(
             nc.vector.tensor_copy(into, xw[z][:].indirect(o1[:, cols]))
 
         def first_layer(h, groups):
-            banks = [psum.tile([P, JH], F32, name="a%d%d" % (t, h), tag="bank%d%d" % (t, h)) for t in range(PACK)]
+            banks = [psum.tile([P, JH], F32, name="a%d%d" % (t, h), tag="a%d" % t) for t in range(PACK)]
             for group in groups:
                 for z, t in [(z, t) for z in range(PASSES) for t in group]:
                     cols = slice(t * P, (t + 1) * P)
@@ -107,7 +106,7 @@ def tile_moe_expert_relay_scattered_pl_kernel(
             for t in range(PACK):
                 nc.scalar.activation(hid[t][:, h * JH : (h + 1) * JH], banks[t][:], RELU)
 
-        xg_first = keep.tile([P, JH], U16, name="xg_first", align_bytes=64)
+        xg_first = keep.tile([P, JH], U16, name="xg_first", tag="xg_then_old", align_bytes=64)
         gather_words(0, 0, xg_first[:])
         nc.vector.tensor_copy(
             wa[:].rearrange("p z (t m) -> p z m t", t=PACK), wa_raw[:].rearrange("p z (m t) -> p z m t", t=PACK)
@@ -115,9 +114,17 @@ def tile_moe_expert_relay_scattered_pl_kernel(
         nc.vector.tensor_copy(
             was[:].rearrange("p z (t m) -> p z t m", t=PACK), was_raw[:].rearrange("p z (m t) -> p z t m", t=PACK)
         )
+        wb_both = keep.tile([P, 3 * N], U8, name="wb_both", tag="wa_then_wb", align_bytes=64)
+        nc.gpsimd.memset(wb_both[:, 2 * N :].bitcast(I32), 0)
+        nc.sync.dma_start(wb_both[:, : 2 * N].bitcast(I32), wb_words[0].bitcast(I32))
+        for q in range(QUADS):
+            nc.sync.dma_start(
+                wb_both[32 * q : 32 * q + 4, 2 * N :].bitcast(I32), wb_scales[0, 4 * q : 4 * q + 4, :].bitcast(I32)
+            )
+
         xg_rest = keep.tile([P, 3 * JH], U16, name="xg_rest", tag="was_then_xg", align_bytes=64)
         gather_words(0, 1, xg_rest[:, :JH])
-        first_layer(0, [(0, 1), (2, 3)])
+        first_layer(0, [(t,) for t in range(PACK)])
         gather_words(1, 0, xg_rest[:, JH : 2 * JH])
         gather_words(1, 1, xg_rest[:, 2 * JH :])
         first_layer(1, [(t,) for t in range(PACK)])
@@ -126,30 +133,37 @@ def tile_moe_expert_relay_scattered_pl_kernel(
                 dealt[:].rearrange("p (t m) -> p t m", t=PACK), raw.rearrange("p (m t) -> p t m", t=PACK)
             )
 
-        old4 = keep.tile([P, PACK, S], F32, name="old4", tag="xw0", align_bytes=64)
-        nc.sync.dma_start(old4[:], old.rearrange("(p t) s -> p t s", t=PACK))
+        pp.append(keep.tile([P, S], F32, name="pp3", tag="was_then_xg", align_bytes=64))
+        nc.gpsimd.memset(pp[3][:], 0.0)
+        old4 = keep.tile([P, PACK * S], F32, name="old4", tag="xg_then_old", align_bytes=64)
+        nc.sync.dma_start(old4[:], old.rearrange("(p t) s -> p (t s)", t=PACK))
 
-        g4 = [keep.tile([P, PACK, IH], F32, name="g4%d" % h, align_bytes=64) for h in range(2)]
-        hb = [keep.tile([P, IH, PACK], BF16, name="hb%d" % h, tag="hb%d" % h, align_bytes=64) for h in range(2)]
+        g_first = keep.tile([P, PACK * IH], F32, name="g_first", align_bytes=64)
+        g4 = [g_first[:], last[:, J:]]
+        hb_second = keep.tile([P, IH * PACK], BF16, name="hb1", tag="hb1", align_bytes=64)
+        hb = [last[:, J + 2 * IH :].bitcast(BF16), hb_second[:]]
         hq = [keep.tile([P, IH], U32, name="hq%d" % h, align_bytes=64) for h in range(2)]
         hs = [keep.tile([P, IH], U8, name="hs%d" % h, align_bytes=64) for h in range(2)]
         ps = [keep.tile([P, I], F32, name="ps%d" % t, align_bytes=64) for t in range(PACK)]
 
         def gather_hid(h, t):
             cols = slice(h * IH // LIST, (h + 1) * IH // LIST)
-            nc.vector.tensor_copy(g4[h][:, t, :], hid[t][:].indirect(o2[:, cols]))
+            window = last[:] if (h, t) == (0, PACK - 1) else hid[t]
+            nc.vector.tensor_copy(g4[h][:, t * IH : (t + 1) * IH], window.indirect(o2[:, cols]))
 
         def weave(h):
             nc.scalar.copy(
-                hb[h][:].rearrange("p (c i) t -> p c t i", i=4), g4[h][:].rearrange("p t (c i) -> p c t i", i=4)
+                hb[h].rearrange("p (c i t) -> p c t i", i=4, t=PACK), g4[h].rearrange("p (t c i) -> p c t i", t=PACK, i=4)
             )
 
         def quantise(h):
-            nc.vector.quantize_mx(out=hq[h][:].bitcast(FP8X4), scales=hs[h][:], in_=hb[h][:].rearrange("p i t -> p (i t)"))
+            nc.vector.quantize_mx(out=hq[h][:].bitcast(FP8X4), scales=hs[h][:], in_=hb[h])
+
+        parked = g4[1][:, :IH]
 
         def second_layer(h, t):
             cols = slice(t * P, (t + 1) * P)
-            bank = psum.tile([P, IH], F32, name="b%d%d" % (t, h), tag="bank%d%d" % (t, h))
+            bank = psum.tile([P, IH], F32, name="b%d%d" % (t, h), tag="b%d" % t)
             nc.tensor.matmul_mx(
                 out=bank[:],
                 lhsT=wb[:, cols].bitcast(FP4X4),
@@ -159,68 +173,73 @@ def tile_moe_expert_relay_scattered_pl_kernel(
                 start=True,
                 stop=True,
             )
-            nc.scalar.copy(ps[t][:, h * IH : (h + 1) * IH], bank[:])
+            nc.scalar.copy(parked if (h, t) == (0, 1) else ps[t][:, h * IH : (h + 1) * IH], bank[:])
 
         def scatter(t, lo, hi):
-            nc.vector.tensor_copy(pp[t][:].indirect(o3[:, lo // LIST : hi // LIST]), ps[t][:, lo:hi])
+            nc.vector.tensor_copy(pp[t][:].indirect(o3[:, lo // LIST : hi // LIST]), parked if (t, lo) == (1, 0) else ps[t][:, lo:hi])
 
-        y4 = keep.tile([P, PACK, S], F32, name="y4", align_bytes=64)
         out_rows = out_0.rearrange("(p t) s -> p t s", t=PACK)
 
         def add_old(t, lo, hi):
-            nc.vector.scalar_tensor_tensor(y4[:, t, lo:hi], old4[:, t, lo:hi], 0.3, pp[t][:, lo:hi], MULT, ADD)
+            nc.vector.scalar_tensor_tensor(y4[:, t * S + lo : t * S + hi], old4[:, t * S + lo : t * S + hi], 0.3, pp[t][:, lo:hi], MULT, ADD)
 
         for t in range(PACK):
             gather_hid(0, t)
         weave(0)
-        for t in range(PACK - 1):
-            gather_hid(1, t)
+        gather_hid(1, 0)
+        gather_hid(1, 1)
         quantise(0)
-        gather_hid(1, PACK - 1)
-        pp = []
-        for t in range(PACK):
-            pp.append(keep.tile([P, S], F32, name="pp%d" % t, tag=["pp0", "pp1", "hid3", "hb0"][t], align_bytes=64))
-            nc.vector.memset(pp[t][:], 0.0)
+        gather_hid(1, 2)
+        gather_hid(1, 3)
         second_layer(0, 0)
-        second_layer(0, 1)
         weave(1)
+        second_layer(0, 1)
         second_layer(0, 2)
         second_layer(0, 3)
         scatter(0, 0, IH)
         quantise(1)
         for t in range(PACK):
             second_layer(1, t)
+        y4 = keep.tile([P, PACK * S], F32, name="y4", tag="hb1", align_bytes=64)
+        for t in range(PACK - 1):
+            nc.scalar.activation(y4[:, (t + 1) * S : (t + 2) * S], old4[:, t * S : (t + 1) * S], COPY, scale=0.3)
+
+        def add_scaled(t):
+            nc.gpsimd.tensor_tensor(y4[:, t * S : (t + 1) * S], y4[:, (t + 1) * S : (t + 2) * S], pp[t][:], ADD)
+
         scatter(1, 0, IH)
         scatter(0, IH, I)
         scatter(1, IH, I)
-        add_old(0, 0, S)
-        nc.sync.dma_start(out_rows[:, 0, :], y4[:, 0, :])
+        add_scaled(0)
+        nc.sync.dma_start(out_rows[:, 0, :], y4[:, 0 * S : 1 * S])
         scatter(2, 0, I)
-        add_old(1, 0, S)
-        nc.sync.dma_start(out_rows[:, 1, :], y4[:, 1, :])
+        add_scaled(1)
+        nc.sync.dma_start(out_rows[:, 1, :], y4[:, 1 * S : 2 * S])
 
-        yb = keep.tile([P, S, PACK], BF16, name="yb", align_bytes=64)
+        half = S // 2
+        yb = [keep.tile([P, half, PACK], BF16, name="yb%d" % c, align_bytes=64) for c in range(2)]
         yq = keep.tile([P, S], U32, name="yq", align_bytes=64)
         ys = keep.tile([P, S], U8, name="ys", align_bytes=64)
 
         def weave_pair(engine_copy, t0, lo, hi):
-            engine_copy(yb[:, lo:hi, t0 : t0 + 2], y4[:, t0 : t0 + 2, lo:hi].rearrange("p t s -> p s t"))
+            c = lo // half
+            pair = y4[:, t0 * S : (t0 + 2) * S].rearrange("p (t s) -> p s t", t=2)
+            engine_copy(yb[c][:, lo - c * half : hi - c * half, t0 : t0 + 2], pair[:, lo:hi, :])
 
-        weave_pair(nc.scalar.copy, 0, 0, S)
+        weave_pair(nc.scalar.copy, 0, 0, half)
+        weave_pair(nc.scalar.copy, 0, half, S)
         scatter(3, 0, I)
-        add_old(2, 0, S)
-        nc.sync.dma_start(out_rows[:, 2, :], y4[:, 2, :])
-        half = S // 2
-        split = 384
-        add_old(3, 0, half)
-        add_old(3, half, S)
-        nc.sync.dma_start(out_rows[:, 3, :], y4[:, 3, :])
-        weave_pair(nc.scalar.copy, 2, 0, split)
-        weave_pair(nc.vector.tensor_copy, 2, split, S)
+        add_scaled(2)
+        nc.sync.dma_start(out_rows[:, 2, :], y4[:, 2 * S : 3 * S])
+        for lo, hi in ((0, half), (half, S)):
+            add_old(3, lo, hi)
+            nc.sync.dma_start(out_rows[:, 3, lo:hi], y4[:, 3 * S + lo : 3 * S + hi])
+        weave_pair(nc.scalar.copy, 2, 0, half)
+        weave_pair(nc.vector.tensor_copy, 2, half, S)
         words = out_1[0].rearrange("p s t -> p (s t)").bitcast(I32)
         for lo, hi in ((half, S), (0, half)):
             nc.vector.quantize_mx(
-                out=yq[:, lo:hi].bitcast(FP8X4), scales=ys[:, lo:hi], in_=yb[:, lo:hi, :].rearrange("p s t -> p (s t)")
+                out=yq[:, lo:hi].bitcast(FP8X4), scales=ys[:, lo:hi], in_=yb[lo // half][:].rearrange("p s t -> p (s t)")
             )
             nc.sync.dma_start(words[:, lo:hi], yq[:, lo:hi].bitcast(I32))
         for q in range(QUADS):

@@ -44,17 +44,16 @@ def tile_moe_expert_relay_scattered_pl_kernel(
         xw = [keep.tile([P, T], U16, name="xw%d" % z, tag="xw%d" % z, align_bytes=64) for z in range(PASSES)]
         wa_raw = keep.tile([P, PASSES, R], I32, name="wa_raw", tag="wa_then_wb", align_bytes=64)
         was_raw = keep.tile([P, PASSES, R], U8, name="was_raw", tag="was_then_xg", align_bytes=64)
-        sg = keep.tile([P, J], U8, name="sg", align_bytes=64)
+        sg = keep.tile([P, J], U8, name="sg", tag="sg_then_pp", align_bytes=64)
         planes = keep.tile([P, PASSES * J], U8, name="planes", align_bytes=64)
 
         nc.gpsimd.memset(was_raw[:].bitcast(I32), 0)
         nc.gpsimd.memset(xs[32:64, :].bitcast(I32), 0)
         nc.gpsimd.memset(xs[64:128, :].bitcast(I32), 0)
-        pp = [keep.tile([P, S], F32, name="pp%d" % t, align_bytes=64) for t in range(PACK - 1)]
+        pp = [keep.tile([P, S], F32, name="pp%d" % t, align_bytes=64) for t in range(2)]
         nc.gpsimd.memset(pp[0][:], 0.0)
         nc.gpsimd.memset(pp[1][:], 0.0)
         nc.gpsimd.memset(planes[:].bitcast(I32), 0)
-        nc.gpsimd.memset(pp[2][:], 0.0)
 
         nc.sync.dma_start(o1[:], offs)
         nc.sync.dma_start(xs[0:32, :].bitcast(I32), xt_scales.rearrange("z q c -> (z q) c").bitcast(I32))
@@ -70,8 +69,8 @@ def tile_moe_expert_relay_scattered_pl_kernel(
         nc.sync.dma_start(o3[:], offs3)
 
         nc.vector.tensor_copy(sg[:], xs[:].indirect(o1[:]))
-        for q in range(QUADS):
-            for z in range(PASSES):
+        for z in reversed(range(PASSES)):
+            for q in range(QUADS):
                 row = 16 * z + 4 * q
                 nc.sync.dma_start(planes[32 * q : 32 * q + 4, z * J : (z + 1) * J].bitcast(I32), sg[row : row + 4, :].bitcast(I32))
 
@@ -106,11 +105,23 @@ def tile_moe_expert_relay_scattered_pl_kernel(
             for t in range(PACK):
                 nc.scalar.activation(hid[t][:, h * JH : (h + 1) * JH], banks[t][:], RELU)
 
-        xg_first = keep.tile([P, JH], U16, name="xg_first", tag="xg_then_old", align_bytes=64)
-        gather_words(0, 0, xg_first[:])
-        nc.vector.tensor_copy(
-            wa[:].rearrange("p z (t m) -> p z m t", t=PACK), wa_raw[:].rearrange("p z (m t) -> p z m t", t=PACK)
+        xg_first = keep.tile([P, 2 * JH], U16, name="xg_first", tag="xg_then_old", align_bytes=64)
+        gather_words(0, 0, xg_first[:, :JH])
+        gather_words(0, 1, xg_first[:, JH:])
+        nc.gpsimd.tensor_copy(
+            wa[:].rearrange("p z (t m) -> p z t m", t=PACK), wa_raw[:].rearrange("p z (m t) -> p z t m", t=PACK)
         )
+        warm = psum.tile([P, JH], F32, name="warm", tag="b3")
+        for z in range(PASSES):
+            nc.tensor.matmul_mx(
+                out=warm[:],
+                lhsT=wa[:, z, :P].bitcast(FP8X4),
+                lhsT_scale=was_raw[:, z, :P],
+                rhs=xg[0, 0].bitcast(FP4X4),
+                rhs_scale=sg[:, :JH],
+                start=True,
+                stop=True,
+            )
         nc.vector.tensor_copy(
             was[:].rearrange("p z (t m) -> p z t m", t=PACK), was_raw[:].rearrange("p z (m t) -> p z t m", t=PACK)
         )
@@ -122,19 +133,19 @@ def tile_moe_expert_relay_scattered_pl_kernel(
                 wb_both[32 * q : 32 * q + 4, 2 * N :].bitcast(I32), wb_scales[0, 4 * q : 4 * q + 4, :].bitcast(I32)
             )
 
-        xg_rest = keep.tile([P, 3 * JH], U16, name="xg_rest", tag="was_then_xg", align_bytes=64)
-        gather_words(0, 1, xg_rest[:, :JH])
+        xg_rest = keep.tile([P, 2 * JH], U16, name="xg_rest", tag="was_then_xg", align_bytes=64)
         first_layer(0, [(t,) for t in range(PACK)])
-        gather_words(1, 0, xg_rest[:, JH : 2 * JH])
-        gather_words(1, 1, xg_rest[:, 2 * JH :])
+        gather_words(1, 0, xg_rest[:, :JH])
+        gather_words(1, 1, xg_rest[:, JH:])
         first_layer(1, [(t,) for t in range(PACK)])
         for dealt, raw in ((wb, wb_both[:, : 2 * N].bitcast(U16)), (wbs, wb_both[:, 2 * N :])):
             nc.vector.tensor_copy(
                 dealt[:].rearrange("p (t m) -> p t m", t=PACK), raw.rearrange("p (m t) -> p t m", t=PACK)
             )
 
-        pp.append(keep.tile([P, S], F32, name="pp3", tag="was_then_xg", align_bytes=64))
-        nc.gpsimd.memset(pp[3][:], 0.0)
+        for t, tag in ((2, "sg_then_pp"), (3, "was_then_xg")):
+            pp.append(keep.tile([P, S], F32, name="pp%d" % t, tag=tag, align_bytes=64))
+            nc.gpsimd.memset(pp[t][:], 0.0)
         old4 = keep.tile([P, PACK * S], F32, name="old4", tag="xg_then_old", align_bytes=64)
         nc.sync.dma_start(old4[:], old.rearrange("(p t) s -> p (t s)", t=PACK))
 

@@ -111,17 +111,6 @@ def tile_moe_expert_relay_scattered_pl_kernel(
         nc.gpsimd.tensor_copy(
             wa[:].rearrange("p z (t m) -> p z t m", t=PACK), wa_raw[:].rearrange("p z (m t) -> p z t m", t=PACK)
         )
-        warm = psum.tile([P, JH], F32, name="warm", tag="b3")
-        for z in range(PASSES):
-            nc.tensor.matmul_mx(
-                out=warm[:],
-                lhsT=wa[:, z, :P].bitcast(FP8X4),
-                lhsT_scale=was_raw[:, z, :P],
-                rhs=xg[0, 0].bitcast(FP4X4),
-                rhs_scale=sg[:, :JH],
-                start=True,
-                stop=True,
-            )
         nc.vector.tensor_copy(
             was[:].rearrange("p z (t m) -> p z t m", t=PACK), was_raw[:].rearrange("p z (m t) -> p z t m", t=PACK)
         )
@@ -228,30 +217,44 @@ def tile_moe_expert_relay_scattered_pl_kernel(
         nc.sync.dma_start(out_rows[:, 1, :], y4[:, 1 * S : 2 * S])
 
         half = S // 2
-        yb = [keep.tile([P, half, PACK], BF16, name="yb%d" % c, align_bytes=64) for c in range(2)]
+        part = S // 4
+        yb = [keep.tile([P, part, PACK], BF16, name="yb%d" % c, align_bytes=64) for c in range(4)]
         yq = keep.tile([P, S], U32, name="yq", align_bytes=64)
         ys = keep.tile([P, S], U8, name="ys", align_bytes=64)
 
-        def weave_pair(engine_copy, t0, lo, hi):
-            c = lo // half
+        def weave_pair(engine_copy, t0, c):
             pair = y4[:, t0 * S : (t0 + 2) * S].rearrange("p (t s) -> p s t", t=2)
-            engine_copy(yb[c][:, lo - c * half : hi - c * half, t0 : t0 + 2], pair[:, lo:hi, :])
+            engine_copy(yb[c][:, :, t0 : t0 + 2], pair[:, c * part : (c + 1) * part, :])
 
-        weave_pair(nc.scalar.copy, 0, 0, half)
-        weave_pair(nc.scalar.copy, 0, half, S)
+        for c in (2, 3, 0, 1):
+            weave_pair(nc.scalar.copy, 0, c)
         scatter(3, 0, I)
         add_scaled(2)
         nc.sync.dma_start(out_rows[:, 2, :], y4[:, 2 * S : 3 * S])
-        for lo, hi in ((0, half), (half, S)):
-            add_old(3, lo, hi)
-            nc.sync.dma_start(out_rows[:, 3, lo:hi], y4[:, 3 * S + lo : 3 * S + hi])
-        weave_pair(nc.scalar.copy, 2, 0, half)
-        weave_pair(nc.vector.tensor_copy, 2, half, S)
+        add_old(3, 0, half)
+        nc.sync.dma_start(out_rows[:, 3, :half], y4[:, 3 * S : 3 * S + half])
+        add_old(3, half, half + part)
+        add_old(3, half + part, S)
+        nc.sync.dma_start(out_rows[:, 3, half:], y4[:, 3 * S + half :])
+        for c in (0, 1):
+            weave_pair(nc.scalar.copy, 2, c)
+        for c in (2, 3):
+            weave_pair(nc.vector.tensor_copy, 2, c)
         words = out_1[0].rearrange("p s t -> p (s t)").bitcast(I32)
-        for lo, hi in ((half, S), (0, half)):
+
+        def quantise_out(c):
+            cols = slice(c * part, (c + 1) * part)
             nc.vector.quantize_mx(
-                out=yq[:, lo:hi].bitcast(FP8X4), scales=ys[:, lo:hi], in_=yb[lo // half][:].rearrange("p s t -> p (s t)")
+                out=yq[:, cols].bitcast(FP8X4), scales=ys[:, cols], in_=yb[c][:].rearrange("p s t -> p (s t)")
             )
-            nc.sync.dma_start(words[:, lo:hi], yq[:, lo:hi].bitcast(I32))
+
+        quantise_out(2)
+        quantise_out(3)
+        nc.sync.dma_start(words[:, half:], yq[:, half:].bitcast(I32))
+        quantise_out(0)
+        nc.sync.dma_start(words[:, :part], yq[:, :part].bitcast(I32))
+        quantise_out(1)
+        nc.sync.dma_start(words[:, part:half], yq[:, part:half].bitcast(I32))
         for q in range(QUADS):
-            nc.scalar.dma_start(out_2[0, 4 * q : 4 * q + 4, :].bitcast(I32), ys[32 * q : 32 * q + 4, :].bitcast(I32))
+            queue = nc.scalar if q % 2 else nc.sync
+            queue.dma_start(out_2[0, 4 * q : 4 * q + 4, :].bitcast(I32), ys[32 * q : 32 * q + 4, :].bitcast(I32))

from contextlib import ExitStack

import concourse.mybir as mybir

K, T, J, I, S, R, N = 1024, 2048, 1024, 512, 1024, 512, 512
FLOPS = 2 * K * R * J + 2 * R * N * I

F32 = mybir.dt.float32
BF16 = mybir.dt.bfloat16
I32 = mybir.dt.int32
U32 = mybir.dt.uint32
U16 = mybir.dt.uint16
U8 = mybir.dt.uint8
FP8X4 = mybir.dt.float8_e4m3fn_x4
FP4X4 = mybir.dt.float4_e2m1fn_x4
MULT = mybir.AluOpType.mult
ADD = mybir.AluOpType.add
COPY = mybir.ActivationFunctionType.Copy
RELU = mybir.ActivationFunctionType.Relu

P = 128
PACK = 4
QUADS = 4
PASSES = K // (P * PACK)
JH = 512
IH = 256
LIST = 16


def tile_moe_expert_relay_scattered_pl_kernel(
    tc, xt_words, xt_scales, wa_words, wa_scales, wb_words, wb_scales, old, offs, offs2, offs3, out_0, out_1, out_2
):
    nc = tc.nc
    with ExitStack() as ctx:
        lists = ctx.enter_context(tc.tile_pool(name="lists", bufs=1))
        keep = ctx.enter_context(tc.tile_pool(name="keep", bufs=1))
        psum = ctx.enter_context(tc.psum_pool(name="psum", bufs=1))

        o1 = lists.tile([P, J // LIST], U16, name="o1")
        o2 = lists.tile([P, I // LIST], U16, name="o2")
        o3 = lists.tile([P, I // LIST], U16, name="o3")

        xs = keep.tile([P, T], U8, name="xs", align_bytes=64)
        xw = [keep.tile([P, T], U16, name="xw%d" % z, tag="xw%d" % z, align_bytes=64) for z in range(PASSES)]
        wa_raw = keep.tile([P, PASSES, R], I32, name="wa_raw", tag="wa_then_wb", align_bytes=64)
        was_raw = keep.tile([P, PASSES, R], U8, name="was_raw", tag="was_then_xg", align_bytes=64)
        sg = keep.tile([P, J], U8, name="sg", tag="sg_then_pp", align_bytes=64)
        planes = keep.tile([P, PASSES * J], U8, name="planes", align_bytes=64)

        nc.gpsimd.memset(was_raw[:].bitcast(I32), 0)
        nc.gpsimd.memset(xs[32:64, :].bitcast(I32), 0)
        nc.gpsimd.memset(xs[64:128, :].bitcast(I32), 0)
        pp = [keep.tile([P, S], F32, name="pp%d" % t, align_bytes=64) for t in range(2)]
        nc.gpsimd.memset(pp[0][:], 0.0)
        nc.gpsimd.memset(pp[1][:], 0.0)
        nc.gpsimd.memset(planes[:].bitcast(I32), 0)

        nc.sync.dma_start(o1[:], offs)
        nc.sync.dma_start(xs[0:32, :].bitcast(I32), xt_scales.rearrange("z q c -> (z q) c").bitcast(I32))
        nc.sync.dma_start(wa_raw[:], wa_words.rearrange("z p n t -> p z (n t)").bitcast(I32))
        for z in range(PASSES):
            nc.sync.dma_start(xw[z][:].bitcast(I32), xt_words[z].bitcast(I32))
        for q in range(QUADS):
            nc.sync.dma_start(
                was_raw[32 * q : 32 * q + 4, :, :].bitcast(I32),
                wa_scales[:, 4 * q : 4 * q + 4, :].rearrange("z q c -> q z c").bitcast(I32),
            )
        nc.sync.dma_start(o2[:], offs2)
        nc.sync.dma_start(o3[:], offs3)

        nc.vector.tensor_copy(sg[:], xs[:].indirect(o1[:]))
        for z in reversed(range(PASSES)):
            for q in range(QUADS):
                row = 16 * z + 4 * q
                nc.sync.dma_start(planes[32 * q : 32 * q + 4, z * J : (z + 1) * J].bitcast(I32), sg[row : row + 4, :].bitcast(I32))

        xg = {}
        wa = keep.tile([P, PASSES, R], I32, name="wa", align_bytes=64)
        was = keep.tile([P, PASSES, R], U8, name="was", align_bytes=64)
        wb = keep.tile([P, N], U16, name="wb", align_bytes=64)
        wbs = keep.tile([P, N], U8, name="wbs", align_bytes=64)
        hid = [keep.tile([P, J], F32, name="hid%d" % t, align_bytes=64)[:] for t in range(PACK - 1)]
        last = keep.tile([P, J + PACK * IH], F32, name="last", align_bytes=64)
        hid.append(last[:, :J])

        def gather_words(h, z, into):
            cols = slice(h * JH // LIST, (h + 1) * JH // LIST)
            xg[h, z] = into
            nc.vector.tensor_copy(into, xw[z][:].indirect(o1[:, cols]))

        def first_layer(h, groups):
            banks = [psum.tile([P, JH], F32, name="a%d%d" % (t, h), tag="a%d" % t) for t in range(PACK)]
            for group in groups:
                for z, t in [(z, t) for z in range(PASSES) for t in group]:
                    cols = slice(t * P, (t + 1) * P)
                    nc.tensor.matmul_mx(
                        out=banks[t][:],
                        lhsT=wa[:, z, cols].bitcast(FP8X4),
                        lhsT_scale=was[:, z, cols],
                        rhs=xg[h, z].bitcast(FP4X4),
                        rhs_scale=planes[:, z * J + h * JH : z * J + (h + 1) * JH],
                        start=(z == 0),
                        stop=(z == PASSES - 1),
                    )
            for t in range(PACK):
                nc.scalar.activation(hid[t][:, h * JH : (h + 1) * JH], banks[t][:], RELU)

        xg_first = keep.tile([P, 2 * JH], U16, name="xg_first", tag="xg_then_old", align_bytes=64)
        gather_words(0, 0, xg_first[:, :JH])
        gather_words(0, 1, xg_first[:, JH:])
        nc.gpsimd.tensor_copy(
            wa[:].rearrange("p z (t m) -> p z t m", t=PACK), wa_raw[:].rearrange("p z (m t) -> p z t m", t=PACK)
        )
        nc.vector.tensor_copy(
            was[:].rearrange("p z (t m) -> p z t m", t=PACK), was_raw[:].rearrange("p z (m t) -> p z t m", t=PACK)
        )
        wb_both = keep.tile([P, 3 * N], U8, name="wb_both", tag="wa_then_wb", align_bytes=64)
        nc.gpsimd.memset(wb_both[:, 2 * N :].bitcast(I32), 0)
        nc.sync.dma_start(wb_both[:, : 2 * N].bitcast(I32), wb_words[0].bitcast(I32))
        for q in range(QUADS):
            nc.sync.dma_start(
                wb_both[32 * q : 32 * q + 4, 2 * N :].bitcast(I32), wb_scales[0, 4 * q : 4 * q + 4, :].bitcast(I32)
            )

        xg_rest = keep.tile([P, 2 * JH], U16, name="xg_rest", tag="was_then_xg", align_bytes=64)
        first_layer(0, [(t,) for t in range(PACK)])
        gather_words(1, 0, xg_rest[:, :JH])
        gather_words(1, 1, xg_rest[:, JH:])
        first_layer(1, [(t,) for t in range(PACK)])
        for dealt, raw in ((wb, wb_both[:, : 2 * N].bitcast(U16)), (wbs, wb_both[:, 2 * N :])):
            nc.vector.tensor_copy(
                dealt[:].rearrange("p (t m) -> p t m", t=PACK), raw.rearrange("p (m t) -> p t m", t=PACK)
            )

        for t, tag in ((2, "sg_then_pp"), (3, "was_then_xg")):
            pp.append(keep.tile([P, S], F32, name="pp%d" % t, tag=tag, align_bytes=64))
            nc.gpsimd.memset(pp[t][:], 0.0)
        old4 = keep.tile([P, PACK * S], F32, name="old4", tag="xg_then_old", align_bytes=64)
        nc.sync.dma_start(old4[:], old.rearrange("(p t) s -> p (t s)", t=PACK))

        g_first = keep.tile([P, PACK * IH], F32, name="g_first", align_bytes=64)
        g4 = [g_first[:], last[:, J:]]
        hb_second = keep.tile([P, IH * PACK], BF16, name="hb1", tag="hb1", align_bytes=64)
        hb = [last[:, J + 2 * IH :].bitcast(BF16), hb_second[:]]
        hq = [keep.tile([P, IH], U32, name="hq%d" % h, align_bytes=64) for h in range(2)]
        hs = [keep.tile([P, IH], U8, name="hs%d" % h, align_bytes=64) for h in range(2)]
        ps = [keep.tile([P, I], F32, name="ps%d" % t, align_bytes=64) for t in range(PACK)]

        def gather_hid(h, t):
            cols = slice(h * IH // LIST, (h + 1) * IH // LIST)
            window = last[:] if (h, t) == (0, PACK - 1) else hid[t]
            nc.vector.tensor_copy(g4[h][:, t * IH : (t + 1) * IH], window.indirect(o2[:, cols]))

        def weave(h):
            nc.scalar.copy(
                hb[h].rearrange("p (c i t) -> p c t i", i=4, t=PACK), g4[h].rearrange("p (t c i) -> p c t i", t=PACK, i=4)
            )

        def quantise(h):
            nc.vector.quantize_mx(out=hq[h][:].bitcast(FP8X4), scales=hs[h][:], in_=hb[h])

        parked = g4[1][:, :IH]

        def second_layer(h, t):
            cols = slice(t * P, (t + 1) * P)
            bank = psum.tile([P, IH], F32, name="b%d%d" % (t, h), tag="b%d" % t)
            nc.tensor.matmul_mx(
                out=bank[:],
                lhsT=wb[:, cols].bitcast(FP4X4),
                lhsT_scale=wbs[:, cols],
                rhs=hq[h][:].bitcast(FP8X4),
                rhs_scale=hs[h][:],
                start=True,
                stop=True,
            )
            nc.scalar.copy(parked if (h, t) == (0, 1) else ps[t][:, h * IH : (h + 1) * IH], bank[:])

        def scatter(t, lo, hi):
            nc.vector.tensor_copy(pp[t][:].indirect(o3[:, lo // LIST : hi // LIST]), parked if (t, lo) == (1, 0) else ps[t][:, lo:hi])

        out_rows = out_0.rearrange("(p t) s -> p t s", t=PACK)

        def add_old(t, lo, hi):
            nc.vector.scalar_tensor_tensor(y4[:, t * S + lo : t * S + hi], old4[:, t * S + lo : t * S + hi], 0.3, pp[t][:, lo:hi], MULT, ADD)

        for t in range(PACK):
            gather_hid(0, t)
        weave(0)
        gather_hid(1, 0)
        gather_hid(1, 1)
        quantise(0)
        gather_hid(1, 2)
        gather_hid(1, 3)
        second_layer(0, 0)
        weave(1)
        second_layer(0, 1)
        second_layer(0, 2)
        second_layer(0, 3)
        scatter(0, 0, IH)
        quantise(1)
        for t in range(PACK):
            second_layer(1, t)
        y4 = keep.tile([P, PACK * S], F32, name="y4", tag="hb1", align_bytes=64)
        for t in range(PACK - 1):
            nc.scalar.activation(y4[:, (t + 1) * S : (t + 2) * S], old4[:, t * S : (t + 1) * S], COPY, scale=0.3)

        def add_scaled(t):
            nc.gpsimd.tensor_tensor(y4[:, t * S : (t + 1) * S], y4[:, (t + 1) * S : (t + 2) * S], pp[t][:], ADD)

        scatter(1, 0, IH)
        scatter(0, IH, I)
        scatter(1, IH, I)
        add_scaled(0)
        nc.sync.dma_start(out_rows[:, 0, :], y4[:, 0 * S : 1 * S])
        scatter(2, 0, I)
        add_scaled(1)
        nc.sync.dma_start(out_rows[:, 1, :], y4[:, 1 * S : 2 * S])

        half = S // 2
        part = S // 4
        yb = [keep.tile([P, part, PACK], BF16, name="yb%d" % c, align_bytes=64) for c in range(4)]
        yq = keep.tile([P, S], U32, name="yq", align_bytes=64)
        ys = keep.tile([P, S], U8, name="ys", align_bytes=64)

        def weave_pair(engine_copy, t0, c):
            pair = y4[:, t0 * S : (t0 + 2) * S].rearrange("p (t s) -> p s t", t=2)
            engine_copy(yb[c][:, :, t0 : t0 + 2], pair[:, c * part : (c + 1) * part, :])

        for c in (2, 3, 0, 1):
            weave_pair(nc.scalar.copy, 0, c)
        scatter(3, 0, I)
        add_scaled(2)
        nc.sync.dma_start(out_rows[:, 2, :], y4[:, 2 * S : 3 * S])
        add_old(3, 0, half)
        nc.sync.dma_start(out_rows[:, 3, :half], y4[:, 3 * S : 3 * S + half])
        add_old(3, half, half + part)
        add_old(3, half + part, S)
        nc.sync.dma_start(out_rows[:, 3, half:], y4[:, 3 * S + half :])
        for c in (0, 1):
            weave_pair(nc.scalar.copy, 2, c)
        for c in (2, 3):
            weave_pair(nc.vector.tensor_copy, 2, c)
        words = out_1[0].rearrange("p s t -> p (s t)").bitcast(I32)

        def quantise_out(c):
            cols = slice(c * part, (c + 1) * part)
            nc.vector.quantize_mx(
                out=yq[:, cols].bitcast(FP8X4), scales=ys[:, cols], in_=yb[c][:].rearrange("p s t -> p (s t)")
            )

        quantise_out(2)
        quantise_out(3)
        nc.sync.dma_start(words[:, half:], yq[:, half:].bitcast(I32))
        quantise_out(0)
        nc.sync.dma_start(words[:, :part], yq[:, :part].bitcast(I32))
        quantise_out(1)
        nc.sync.dma_start(words[:, part:half], yq[:, part:half].bitcast(I32))
        for q in range(QUADS):
            queue = nc.scalar if q % 2 else nc.sync
            queue.dma_start(out_2[0, 4 * q : 4 * q + 4, :].bitcast(I32), ys[32 * q : 32 * q + 4, :].bitcast(I32))
